import numpy as np
import ml_dtypes


def mxq(x, axis, fmt="e4m3"):
    dtype, down = {"e4m3": (ml_dtypes.float8_e4m3fn, 7), "e5m2": (ml_dtypes.float8_e5m2, 14)}[fmt]
    v = np.moveaxis(np.asarray(x, np.float32).astype(ml_dtypes.bfloat16).astype(np.float64), axis, -1)
    blocks = v.reshape(v.shape[:-1] + (-1, 32))
    amax = np.abs(blocks).max(-1, keepdims=True)
    byte = np.maximum(np.where(amax > 0, np.frexp(amax)[1] - 1 + 127, 0) - down, 1)
    scale = np.exp2(byte - 127.0)
    codes = (blocks / scale).astype(np.float32).astype(dtype).astype(np.float64)
    return np.moveaxis((codes * scale).reshape(v.shape), -1, axis)


WIDE = False


def mx_kscale(k):
    if not WIDE:
        return np.ones(k)
    levels = np.array([10, -10, 5, -5, 0])
    if k % 512:
        return np.exp2(np.random.permutation(np.resize(levels, k // 32))).repeat(32)
    a = np.empty((k // 512, 16))
    for p in range(k // 512):
        a[p, :8] = np.random.permutation(np.resize(levels, 8))
        for g in range(8):
            far = levels[np.abs(levels - a[p, g]) >= 10]
            a[p, g + 8] = far[np.random.randint(len(far))]
    return np.exp2(a.ravel()).repeat(32)


def f64(x):
    return np.asarray(x).astype(np.float64)


E2M1 = np.array([0.0, 0.5, 1.0, 1.5, 2.0, 3.0, 4.0, 6.0, -0.0, -0.5, -1.0, -1.5, -2.0, -3.0, -4.0, -6.0])


def pack_weight(w, fmt):
    k, n = w.shape
    w = f64(np.asarray(w, np.float32).astype(ml_dtypes.bfloat16)).reshape(k // 32, 32, n)
    amax = np.abs(w).max(1)
    if fmt == "e4m3":
        byte = np.frexp(amax)[1] - 1 + 127 - 7
    else:
        mant, ex = np.frexp(amax / 6.0)
        byte = np.where(mant > 0.5, ex, ex - 1) + 127
    byte = np.clip(np.where(amax > 0, byte, 1), 1, 254)
    scaled = (w * np.exp2(127.0 - byte)[:, None, :]).reshape(k, n).astype(np.float32)
    by_word = np.ascontiguousarray(scaled.reshape(k // 512, 128, 4, n).transpose(0, 1, 3, 2))
    if fmt == "e4m3":
        words = by_word.astype(ml_dtypes.float8_e4m3fn).view(np.uint8)
    else:
        c = by_word.astype(ml_dtypes.float4_e2m1fn).view(np.uint8) & 0xF
        words = (c[..., 0::2] | (c[..., 1::2] << 4)).reshape(k // 512, 128, 2 * n)
    return np.ascontiguousarray(words), np.ascontiguousarray(byte.astype(np.uint8).reshape(k // 512, 16, n))


def unpack_weight(words, scales, fmt):
    g, _, n = scales.shape
    words = np.ascontiguousarray(words).reshape(g, 128, n, -1)
    if fmt == "e4m3":
        vals = words.view(ml_dtypes.float8_e4m3fn).astype(np.float64)
    else:
        nib = np.empty((g, 128, n, 4), np.uint8)
        nib[..., 0::2] = words & 0xF
        nib[..., 1::2] = words >> 4
        vals = E2M1[nib]
    vals = vals * np.repeat(np.exp2(scales.astype(np.float64) - 127.0), 8, axis=1)[..., None]
    return vals.transpose(0, 1, 3, 2).reshape(g * 512, n)


def bf(x):
    return np.asarray(x, np.float32).astype(ml_dtypes.bfloat16)


def planes(Y):
    r, m = Y.shape
    b = f64(bf(Y)).reshape(r // 32, 32, m)
    amax = np.abs(b).max(1)
    byte = np.clip(np.where(amax > 0, np.frexp(amax)[1] - 1 + 127 - 7, 1), 1, 254)
    codes = (b * np.exp2(127.0 - byte)[:, None, :]).reshape(r, m).astype(np.float32).astype(ml_dtypes.float8_e4m3fn).view(np.uint8)
    words = codes.reshape(r // 512, 128, 4, m).transpose(0, 1, 3, 2)
    return np.ascontiguousarray(words), np.ascontiguousarray(byte.astype(np.uint8).reshape(r // 512, 16, m))


K, L, T, R, N = 1024, 1024, 512, 512, 512


def setup_inputs():
    n = np.random.standard_normal
    fk = mx_kscale(K)
    fr = mx_kscale(R)
    fl = mx_kscale(L)
    xtp = pack_weight(n((K, T)) / fk[:, None], "e2m1")
    wap = pack_weight(n((K, R)) * 1 / np.sqrt(K) * fk[:, None] * fr, "e4m3")
    wbp = pack_weight(n((R, N)) * 1 / np.sqrt(R) / fr[:, None], "e2m1")
    xqp = pack_weight(n((L, T)) / fl[:, None], "e4m3")
    wqp = pack_weight(n((L, N)) * 1 / np.sqrt(L) * fl[:, None], "e2m1")
    return {
        "xt_words": xtp[0],
        "xt_scales": xtp[1],
        "wa_words": wap[0],
        "wa_scales": wap[1],
        "wb_words": wbp[0],
        "wb_scales": wbp[1],
        "xq_words": xqp[0],
        "xq_scales": xqp[1],
        "wq_words": wqp[0],
        "wq_scales": wqp[1],
        "tg": (1.0 * n((N, T))).astype(np.float32),
    }


def reference(xt_words, xt_scales, wa_words, wa_scales, wb_words, wb_scales, xq_words, xq_scales, wq_words, wq_scales, tg):
    xtu = unpack_weight(xt_words, xt_scales, "e2m1")
    wau = unpack_weight(wa_words, wa_scales, "e4m3")
    wbu = unpack_weight(wb_words, wb_scales, "e2m1")
    xqu = unpack_weight(xq_words, xq_scales, "e4m3")
    wqu = unpack_weight(wq_words, wq_scales, "e2m1")
    a = wau.T @ xtu
    hid = np.maximum(a, 0.0)
    hidq = mxq(hid, 0, "e4m3")
    p = wbu.T @ hidq + wqu.T @ xqu
    y = np.tanh(f64(tg) - p)
    words, scales = planes(y)
    return y, words, scales

@@ -1,0 +1,227 @@
+from contextlib import ExitStack
+
+import concourse.mybir as mybir
+
+K, L, T, R, N = 1024, 1024, 512, 512, 512
+FLOPS = 2 * T * (K * R + R * N + L * N)
+
+F32 = mybir.dt.float32
+BF16 = mybir.dt.bfloat16
+I32 = mybir.dt.int32
+U8 = mybir.dt.uint8
+FP8X4 = mybir.dt.float8_e4m3fn_x4
+FP4X4 = mybir.dt.float4_e2m1fn_x4
+ACT = mybir.ActivationFunctionType
+ALU = mybir.AluOpType
+
+P = 128
+PACK = 4
+W = 512
+CH = 128
+
+
+def tile_mix_unexplained_rest_pl_kernel(
+    tc, xt_words, xt_scales, wa_words, wa_scales, wb_words, wb_scales,
+    xq_words, xq_scales, wq_words, wq_scales, tg, out_0, out_1, out_2,
+):
+    nc = tc.nc
+    with ExitStack() as ctx:
+        sb = ctx.enter_context(tc.tile_pool(name="sb", bufs=1))
+        ps = ctx.enter_context(tc.psum_pool(name="ps", bufs=1))
+        ctx.enter_context(tc.manual_schedule())
+
+        def tile(name, shape, dtype):
+            return sb.tile(shape, dtype, name=name, align_bytes=64)
+
+        wa_w_raw = tile("wa_w_raw", [P, 2, W], I32)
+        wa_w = [tile("wa_w%d" % z, [P, W], I32) for z in range(2)]
+        wa_s_raw = tile("wa_s_raw", [P, 2, W], U8)
+        wa_s = tile("wa_s", [P, 2, W], U8)
+        xt_w = tile("xt_w", [P, 2, 2 * W], U8)
+        xt_s = tile("xt_s", [P, 2, W], U8)
+        wq_w_raw = tile("wq_w_raw", [P, 2, 2 * W], U8)
+        wq_w = [tile("wq_w%d" % z, [P, 2 * W], U8) for z in range(2)]
+        wq_s_raw = tile("wq_s_raw", [P, 2, W], U8)
+        wq_s = tile("wq_s", [P, 2, W], U8)
+        xq_w = tile("xq_w", [P, 2, W], I32)
+        xq_s = tile("xq_s", [P, 2, W], U8)
+        wb_w_raw = tile("wb_w_raw", [P, 1, 2 * W], U8)
+        wb_w = tile("wb_w", [P, 2 * W], U8)
+        wb_s_raw = tile("wb_s_raw", [P, 1, W], U8)
+        wb_s = tile("wb_s", [P, 1, W], U8)
+        tg_sb = [tile("tg%d" % h, [P, 2, T], F32) for h in range(2)]
+        hid = [tile("hid%d" % c, [P, CH, PACK], BF16) for c in range(4)]
+        hid_w = tile("hid_w", [P, T], I32)
+        hid_s = tile("hid_s", [P, T], U8)
+        rest = [tile("rest%d" % j, [P, T], F32) for j in range(PACK)]
+        y = tile("y", [P, PACK, T], F32)
+        y_bf = [tile("y_bf%d" % h, [P, T // 2, PACK], BF16) for h in range(2)]
+        y_w = tile("y_w", [P, T], I32)
+        y_s = tile("y_s", [P, T], U8)
+        warm = tile("warm", [P, 8], F32)
+
+        a_ps = [ps.tile([P, PACK, CH], F32, name="a_ps%d" % c) for c in range(4)]
+        p_ps = [ps.tile([P, T], F32, name="p_ps%d" % j) for j in range(PACK)]
+
+        def zero(plane):
+            nc.vector.memset(plane[:].bitcast(I32), 0)
+
+        def load_scale_rows(queue, plane, scales, q):
+            queue.dma_start(
+                out=plane[32 * q : 32 * q + 4, :, :].bitcast(I32),
+                in_=scales[:, 4 * q : 4 * q + 4, :].rearrange("z r c -> r z c").bitcast(I32),
+            )
+
+        def load_fp8_words(dst, words):
+            nc.sync.dma_start(out=dst[:], in_=words.rearrange("z p c b -> p z (c b)").bitcast(I32))
+
+        def load_fp4_words(dst, words):
+            nc.sync.dma_start(out=dst[:].bitcast(I32), in_=words.rearrange("z p c -> p z c").bitcast(I32))
+
+        def deal_scales(dst, src):
+            nc.vector.tensor_copy(
+                out=dst[:].rearrange("p z (j m) -> p z j m", j=PACK),
+                in_=src[:].rearrange("p z (m j) -> p z j m", j=PACK),
+            )
+
+        def deal_fp8_words(dst, src):
+            nc.vector.tensor_copy(
+                out=dst.rearrange("p (j g i) -> p g j i", j=PACK, i=2),
+                in_=src.rearrange("p (g i j) -> p g j i", j=PACK, i=2),
+            )
+
+        def deal_fp4_words(dst, src):
+            nc.vector.tensor_copy(
+                out=dst.rearrange("p (j m b) -> p j m b", j=PACK, b=2),
+                in_=src.rearrange("p (m j b) -> p j m b", j=PACK, b=2),
+            )
+
+        for plane in (wa_s_raw, xt_s, wb_s_raw, wq_s_raw, xq_s):
+            zero(plane)
+        nc.vector.memset(warm[:], 0.0)
+        for q in range(4):
+            load_scale_rows(nc.scalar, wa_s_raw, wa_scales, q)
+        load_fp8_words(wa_w_raw, wa_words)
+        load_fp4_words(xt_w, xt_words)
+        for q in range(4):
+            load_scale_rows(nc.sync, xt_s, xt_scales, q)
+        for q in range(4):
+            load_scale_rows(nc.gpsimd, wb_s_raw, wb_scales, q)
+        nc.scalar.activation(out=warm[:, 4:5], in_=warm[:, 0:1], func=ACT.Tanh)
+        load_fp4_words(wq_w_raw, wq_words)
+        load_fp8_words(xq_w, xq_words)
+        for q in range(4):
+            load_scale_rows(nc.sync, wq_s_raw, wq_scales, q)
+        load_fp4_words(wb_w_raw, wb_words)
+        tg_rows = tg.rearrange("(p j) t -> p j t", j=PACK)
+        nc.sync.dma_start(out=tg_sb[0][:], in_=tg_rows[:, 0:2, :])
+        for q in range(4):
+            load_scale_rows(nc.sync, xq_s, xq_scales, q)
+        nc.sync.dma_start(out=tg_sb[1][:], in_=tg_rows[:, 2:4, :])
+
+        deal_scales(wa_s, wa_s_raw)
+        for z in range(2):
+            deal_fp8_words(wa_w[z][:], wa_w_raw[:, z, :])
+        for c in range(4):
+            for z in range(2):
+                for j in range(PACK):
+                    nc.tensor.matmul_mx(
+                        out=a_ps[c][:, j, :],
+                        lhsT=wa_w[z][:, P * j : P * (j + 1)].bitcast(FP8X4),
+                        lhsT_scale=wa_s[:, z, P * j : P * (j + 1)],
+                        rhs=xt_w[:, z, 2 * CH * c : 2 * CH * (c + 1)].bitcast(FP4X4),
+                        rhs_scale=xt_s[:, z, CH * c : CH * (c + 1)],
+                        start=(z == 0 and j == 0),
+                        stop=(z == 1 and j == PACK - 1),
+                    )
+            nc.scalar.activation(out=hid[c][:], in_=a_ps[c][:].rearrange("p j t -> p t j"), func=ACT.Relu)
+
+        def quantize_hid(c):
+            nc.vector.quantize_mx(
+                out=hid_w[:, CH * c : CH * (c + 1)].bitcast(FP8X4),
+                scales=hid_s[:, CH * c : CH * (c + 1)],
+                in_=hid[c][:].rearrange("p t j -> p (t j)"),
+            )
+
+        deal_fp4_words(wq_w[0][:], wq_w_raw[:, 0, :])
+        deal_fp4_words(wq_w[1][:], wq_w_raw[:, 1, :])
+        deal_scales(wq_s, wq_s_raw)
+        quantize_hid(0)
+        deal_fp4_words(wb_w[:], wb_w_raw[:, 0, :])
+        quantize_hid(1)
+        deal_scales(wb_s, wb_s_raw)
+        quantize_hid(2)
+        quantize_hid(3)
+
+        def wq_passes(j):
+            for z in range(2):
+                nc.tensor.matmul_mx(
+                    out=p_ps[j][:],
+                    lhsT=wq_w[z][:, 2 * P * j : 2 * P * (j + 1)].bitcast(FP4X4),
+                    lhsT_scale=wq_s[:, z, P * j : P * (j + 1)],
+                    rhs=xq_w[:, z, :].bitcast(FP8X4),
+                    rhs_scale=xq_s[:, z, :],
+                    start=(z == 0),
+                    stop=False,
+                )
+
+        def wb_pass(j):
+            nc.tensor.matmul_mx(
+                out=p_ps[j][:],
+                lhsT=wb_w[:, 2 * P * j : 2 * P * (j + 1)].bitcast(FP4X4),
+                lhsT_scale=wb_s[:, 0, P * j : P * (j + 1)],
+                rhs=hid_w[:].bitcast(FP8X4),
+                rhs_scale=hid_s[:],
+                start=False,
+                stop=True,
+            )
+
+        wq_passes(0)
+        wq_passes(1)
+        wb_pass(0)
+        wb_pass(1)
+        for j in range(2, PACK):
+            wq_passes(j)
+            wb_pass(j)
+
+        out_rows = out_0.rearrange("(p j) t -> p j t", j=PACK)
+
+        def squash(j, cols):
+            nc.vector.tensor_tensor(
+                out=rest[j][:, cols], in0=tg_sb[j // 2][:, j % 2, cols], in1=p_ps[j][:, cols], op=ALU.subtract
+            )
+            nc.scalar.activation(out=y[:, j, cols], in_=rest[j][:, cols], func=ACT.Tanh)
+
+        for j in range(PACK - 1):
+            squash(j, slice(0, T))
+            nc.sync.dma_start(out=out_rows[:, j, :], in_=y[:, j, :])
+        for h in range(2):
+            squash(PACK - 1, slice(h * T // 2, (h + 1) * T // 2))
+        nc.sync.dma_start(out=out_rows[:, PACK - 1, :], in_=y[:, PACK - 1, :])
+
+        def round_views(c):
+            dst = y_bf[c // 2][:, CH * (c % 2) : CH * (c % 2 + 1), :].rearrange("p (g i) j -> p g j i", i=4)
+            src = y[:, :, CH * c : CH * (c + 1)].rearrange("p j (g i) -> p g j i", i=4)
+            return dst, src
+
+        def quantize_y(h):
+            cols = slice(h * T // 2, (h + 1) * T // 2)
+            nc.vector.quantize_mx(
+                out=y_w[:, cols].bitcast(FP8X4), scales=y_s[:, cols], in_=y_bf[h][:].rearrange("p t j -> p (t j)")
+            )
+
+        out_words = out_1.rearrange("z p c b -> p (z c b)").bitcast(I32)
+        for c in range(3):
+            dst, src = round_views(c)
+            nc.vector.tensor_copy(out=dst, in_=src)
+        dst, src = round_views(3)
+        nc.scalar.copy(out=dst, in_=src)
+        for h in range(2):
+            quantize_y(h)
+            cols = slice(h * T // 2, (h + 1) * T // 2)
+            nc.sync.dma_start(out=out_words[:, cols], in_=y_w[:, cols])
+        for q in range(4):
+            queue = nc.scalar if q % 2 == 0 else nc.sync
+            queue.dma_start(
+                out=out_2[0, 4 * q : 4 * q + 4, :].bitcast(I32), in_=y_s[32 * q : 32 * q + 4, :].bitcast(I32)
+            )

@@ -33,7 +33,7 @@ def tile_mix_unexplained_rest_pl_kernel(
         def tile(name, shape, dtype):
             return sb.tile(shape, dtype, name=name, align_bytes=64)
 
-        wa_w_raw = tile("wa_w_raw", [P, 2, W], I32)
+        wa_w_raw = [tile("wa_w_raw%d" % z, [P, 1, W], I32) for z in range(2)]
         wa_w = [tile("wa_w%d" % z, [P, W], I32) for z in range(2)]
         wa_s_raw = tile("wa_s_raw", [P, 2, W], U8)
         wa_s = tile("wa_s", [P, 2, W], U8)
@@ -96,32 +96,51 @@ def tile_mix_unexplained_rest_pl_kernel(
                 in_=src.rearrange("p (m j b) -> p j m b", j=PACK, b=2),
             )
 
-        for plane in (wa_s_raw, xt_s, wb_s_raw, wq_s_raw, xq_s):
+        for plane in (wa_s_raw, xt_s, wq_s_raw, wb_s_raw, xq_s):
             zero(plane)
         nc.vector.memset(warm[:], 0.0)
-        for q in range(4):
+        load_fp8_words(wa_w_raw[0], wa_words[0:1])
+        load_scale_rows(nc.sync, wa_s_raw, wa_scales, 0)
+        for q in range(1, 4):
             load_scale_rows(nc.scalar, wa_s_raw, wa_scales, q)
-        load_fp8_words(wa_w_raw, wa_words)
+        load_scale_rows(nc.sync, xt_s, xt_scales, 0)
+        load_fp8_words(wa_w_raw[1], wa_words[1:2])
         load_fp4_words(xt_w, xt_words)
-        for q in range(4):
-            load_scale_rows(nc.sync, xt_s, xt_scales, q)
-        for q in range(4):
-            load_scale_rows(nc.gpsimd, wb_s_raw, wb_scales, q)
         nc.scalar.activation(out=warm[:, 4:5], in_=warm[:, 0:1], func=ACT.Tanh)
+        for q in range(2, 4):
+            load_scale_rows(nc.gpsimd, wq_s_raw, wq_scales, q)
+        for q in range(2):
+            load_scale_rows(nc.gpsimd, wb_s_raw, wb_scales, q)
+        load_scale_rows(nc.sync, xt_s, xt_scales, 1)
+        load_scale_rows(nc.scalar, xt_s, xt_scales, 2)
+        load_scale_rows(nc.sync, xt_s, xt_scales, 3)
+        for q in range(2):
+            load_scale_rows(nc.scalar, wq_s_raw, wq_scales, q)
+        load_fp4_words(wb_w_raw, wb_words)
         load_fp4_words(wq_w_raw, wq_words)
         load_fp8_words(xq_w, xq_words)
         for q in range(4):
-            load_scale_rows(nc.sync, wq_s_raw, wq_scales, q)
-        load_fp4_words(wb_w_raw, wb_words)
+            load_scale_rows(nc.sync, xq_s, xq_scales, q)
+        for q in range(2, 4):
+            load_scale_rows(nc.sync, wb_s_raw, wb_scales, q)
         tg_rows = tg.rearrange("(p j) t -> p j t", j=PACK)
         nc.sync.dma_start(out=tg_sb[0][:], in_=tg_rows[:, 0:2, :])
-        for q in range(4):
-            load_scale_rows(nc.sync, xq_s, xq_scales, q)
         nc.sync.dma_start(out=tg_sb[1][:], in_=tg_rows[:, 2:4, :])
 
+        for i in range(11):
+            nc.tensor.matmul_mx(
+                out=a_ps[3][:, i % PACK, :],
+                lhsT=wa_w_raw[0][:, 0, 0:P].bitcast(FP8X4),
+                lhsT_scale=wa_s_raw[:, 0, 0:P],
+                rhs=wa_w_raw[0][:, 0, P : P + CH // 2].bitcast(U8).bitcast(FP4X4),
+                rhs_scale=wa_s_raw[:, 0, P : P + CH],
+                start=True,
+                stop=True,
+            )
+
+        deal_fp8_words(wa_w[0][:], wa_w_raw[0][:, 0, :])
         deal_scales(wa_s, wa_s_raw)
-        for z in range(2):
-            deal_fp8_words(wa_w[z][:], wa_w_raw[:, z, :])
+        deal_fp8_words(wa_w[1][:], wa_w_raw[1][:, 0, :])
         for c in range(4):
             for z in range(2):
                 for j in range(PACK):
@@ -143,27 +162,26 @@ def tile_mix_unexplained_rest_pl_kernel(
                 in_=hid[c][:].rearrange("p t j -> p (t j)"),
             )
 
+        deal_fp4_words(wb_w[:], wb_w_raw[:, 0, :])
+        deal_scales(wq_s, wq_s_raw)
         deal_fp4_words(wq_w[0][:], wq_w_raw[:, 0, :])
         deal_fp4_words(wq_w[1][:], wq_w_raw[:, 1, :])
-        deal_scales(wq_s, wq_s_raw)
         quantize_hid(0)
-        deal_fp4_words(wb_w[:], wb_w_raw[:, 0, :])
         quantize_hid(1)
-        deal_scales(wb_s, wb_s_raw)
         quantize_hid(2)
+        deal_scales(wb_s, wb_s_raw)
         quantize_hid(3)
 
-        def wq_passes(j):
-            for z in range(2):
-                nc.tensor.matmul_mx(
-                    out=p_ps[j][:],
-                    lhsT=wq_w[z][:, 2 * P * j : 2 * P * (j + 1)].bitcast(FP4X4),
-                    lhsT_scale=wq_s[:, z, P * j : P * (j + 1)],
-                    rhs=xq_w[:, z, :].bitcast(FP8X4),
-                    rhs_scale=xq_s[:, z, :],
-                    start=(z == 0),
-                    stop=False,
-                )
+        def wq_pass(j, z):
+            nc.tensor.matmul_mx(
+                out=p_ps[j][:],
+                lhsT=wq_w[z][:, 2 * P * j : 2 * P * (j + 1)].bitcast(FP4X4),
+                lhsT_scale=wq_s[:, z, P * j : P * (j + 1)],
+                rhs=xq_w[:, z, :].bitcast(FP8X4),
+                rhs_scale=xq_s[:, z, :],
+                start=(z == 0),
+                stop=False,
+            )
 
         def wb_pass(j):
             nc.tensor.matmul_mx(
@@ -176,13 +194,17 @@ def tile_mix_unexplained_rest_pl_kernel(
                 stop=True,
             )
 
-        wq_passes(0)
-        wq_passes(1)
-        wb_pass(0)
-        wb_pass(1)
-        for j in range(2, PACK):
-            wq_passes(j)
+        for j in range(3):
+            wq_pass(j, 0)
+        for j in range(2):
+            wq_pass(j, 1)
+        for j in range(2):
             wb_pass(j)
+        wq_pass(2, 1)
+        wb_pass(2)
+        wq_pass(3, 0)
+        wq_pass(3, 1)
+        wb_pass(3)
 
         out_rows = out_0.rearrange("(p j) t -> p j t", j=PACK)
 
@@ -195,8 +217,8 @@ def tile_mix_unexplained_rest_pl_kernel(
         for j in range(PACK - 1):
             squash(j, slice(0, T))
             nc.sync.dma_start(out=out_rows[:, j, :], in_=y[:, j, :])
-        for h in range(2):
-            squash(PACK - 1, slice(h * T // 2, (h + 1) * T // 2))
+        for cols in (slice(0, CH), slice(CH, 2 * CH), slice(2 * CH, T)):
+            squash(PACK - 1, cols)
         nc.sync.dma_start(out=out_rows[:, PACK - 1, :], in_=y[:, PACK - 1, :])
 
         def round_views(c):

@@ -49,7 +49,8 @@ def tile_mix_unexplained_rest_pl_kernel(
         wb_w = tile("wb_w", [P, 2 * W], U8)
         wb_s_raw = tile("wb_s_raw", [P, 1, W], U8)
         wb_s = tile("wb_s", [P, 1, W], U8)
-        tg_sb = [tile("tg%d" % h, [P, 2, T], F32) for h in range(2)]
+        tg_sb = [tile("tg%d" % h, [P, rows, T], F32) for h, rows in enumerate((2, 1, 1))]
+        tg_of = [tg_sb[0][:, 0, :], tg_sb[0][:, 1, :], tg_sb[1][:, 0, :], tg_sb[2][:, 0, :]]
         hid = [tile("hid%d" % c, [P, CH, PACK], BF16) for c in range(4)]
         hid_w = tile("hid_w", [P, T], I32)
         hid_s = tile("hid_s", [P, T], U8)
@@ -60,8 +61,8 @@ def tile_mix_unexplained_rest_pl_kernel(
         y_s = tile("y_s", [P, T], U8)
         warm = tile("warm", [P, 8], F32)
 
-        a_ps = [ps.tile([P, PACK, CH], F32, name="a_ps%d" % c) for c in range(4)]
-        p_ps = [ps.tile([P, T], F32, name="p_ps%d" % j) for j in range(PACK)]
+        a_ps = [ps.tile([P, PACK, CH], F32, name="a_ps%d" % c, tag="chunk%d" % c) for c in range(4)]
+        p_ps = [ps.tile([P, T], F32, name="p_ps%d" % j) for j in range(PACK - 1)]
 
         def zero(plane):
             nc.vector.memset(plane[:].bitcast(I32), 0)
@@ -96,28 +97,26 @@ def tile_mix_unexplained_rest_pl_kernel(
                 in_=src.rearrange("p (m j b) -> p j m b", j=PACK, b=2),
             )
 
-        for plane in (wa_s_raw, xt_s, wq_s_raw, wb_s_raw, xq_s):
+        nc.gpsimd.memset(wq_s_raw[:].bitcast(I32), 0)
+        for plane in (wa_s_raw, xt_s, wb_s_raw, xq_s):
             zero(plane)
         nc.vector.memset(warm[:], 0.0)
         load_fp8_words(wa_w_raw[0], wa_words[0:1])
-        load_scale_rows(nc.sync, wa_s_raw, wa_scales, 0)
-        for q in range(1, 4):
-            load_scale_rows(nc.scalar, wa_s_raw, wa_scales, q)
-        load_scale_rows(nc.sync, xt_s, xt_scales, 0)
+        for q in range(4):
+            load_scale_rows(nc.sync if q < 2 else nc.scalar, wa_s_raw, wa_scales, q)
         load_fp8_words(wa_w_raw[1], wa_words[1:2])
         load_fp4_words(xt_w, xt_words)
+        load_fp4_words(wq_w_raw, wq_words)
         nc.scalar.activation(out=warm[:, 4:5], in_=warm[:, 0:1], func=ACT.Tanh)
         for q in range(2, 4):
             load_scale_rows(nc.gpsimd, wq_s_raw, wq_scales, q)
         for q in range(2):
             load_scale_rows(nc.gpsimd, wb_s_raw, wb_scales, q)
-        load_scale_rows(nc.sync, xt_s, xt_scales, 1)
-        load_scale_rows(nc.scalar, xt_s, xt_scales, 2)
-        load_scale_rows(nc.sync, xt_s, xt_scales, 3)
-        for q in range(2):
-            load_scale_rows(nc.scalar, wq_s_raw, wq_scales, q)
+        for q in range(4):
+            load_scale_rows(nc.sync if q < 3 else nc.scalar, xt_s, xt_scales, q)
+        load_scale_rows(nc.scalar, wq_s_raw, wq_scales, 0)
         load_fp4_words(wb_w_raw, wb_words)
-        load_fp4_words(wq_w_raw, wq_words)
+        load_scale_rows(nc.sync, wq_s_raw, wq_scales, 1)
         load_fp8_words(xq_w, xq_words)
         for q in range(4):
             load_scale_rows(nc.sync, xq_s, xq_scales, q)
@@ -125,7 +124,8 @@ def tile_mix_unexplained_rest_pl_kernel(
             load_scale_rows(nc.sync, wb_s_raw, wb_scales, q)
         tg_rows = tg.rearrange("(p j) t -> p j t", j=PACK)
         nc.sync.dma_start(out=tg_sb[0][:], in_=tg_rows[:, 0:2, :])
-        nc.sync.dma_start(out=tg_sb[1][:], in_=tg_rows[:, 2:4, :])
+        nc.sync.dma_start(out=tg_sb[1][:], in_=tg_rows[:, 2:3, :])
+        nc.sync.dma_start(out=tg_sb[2][:], in_=tg_rows[:, 3:4, :])
 
         for i in range(11):
             nc.tensor.matmul_mx(
@@ -162,63 +162,70 @@ def tile_mix_unexplained_rest_pl_kernel(
                 in_=hid[c][:].rearrange("p t j -> p (t j)"),
             )
 
-        deal_fp4_words(wb_w[:], wb_w_raw[:, 0, :])
-        deal_scales(wq_s, wq_s_raw)
         deal_fp4_words(wq_w[0][:], wq_w_raw[:, 0, :])
         deal_fp4_words(wq_w[1][:], wq_w_raw[:, 1, :])
+        deal_fp4_words(wb_w[:], wb_w_raw[:, 0, :])
+        deal_scales(wq_s, wq_s_raw)
         quantize_hid(0)
         quantize_hid(1)
         quantize_hid(2)
         deal_scales(wb_s, wb_s_raw)
         quantize_hid(3)
 
-        def wq_pass(j, z):
+        def wq_pass(acc, j, z, cols):
             nc.tensor.matmul_mx(
-                out=p_ps[j][:],
+                out=acc,
                 lhsT=wq_w[z][:, 2 * P * j : 2 * P * (j + 1)].bitcast(FP4X4),
                 lhsT_scale=wq_s[:, z, P * j : P * (j + 1)],
-                rhs=xq_w[:, z, :].bitcast(FP8X4),
-                rhs_scale=xq_s[:, z, :],
+                rhs=xq_w[:, z, cols].bitcast(FP8X4),
+                rhs_scale=xq_s[:, z, cols],
                 start=(z == 0),
                 stop=False,
             )
 
-        def wb_pass(j):
+        def wb_pass(acc, j, cols, stop):
             nc.tensor.matmul_mx(
-                out=p_ps[j][:],
+                out=acc,
                 lhsT=wb_w[:, 2 * P * j : 2 * P * (j + 1)].bitcast(FP4X4),
                 lhsT_scale=wb_s[:, 0, P * j : P * (j + 1)],
-                rhs=hid_w[:].bitcast(FP8X4),
-                rhs_scale=hid_s[:],
+                rhs=hid_w[:, cols].bitcast(FP8X4),
+                rhs_scale=hid_s[:, cols],
                 start=False,
-                stop=True,
+                stop=stop,
             )
 
-        for j in range(3):
-            wq_pass(j, 0)
-        for j in range(2):
-            wq_pass(j, 1)
-        for j in range(2):
-            wb_pass(j)
-        wq_pass(2, 1)
-        wb_pass(2)
-        wq_pass(3, 0)
-        wq_pass(3, 1)
-        wb_pass(3)
+        whole = slice(0, T)
+        halves = [slice(0, T // 2), slice(T // 2, T)]
+        chunks = [slice(CH * c, CH * (c + 1)) for c in range(4)]
+        for z in range(2):
+            for j in range(2):
+                wq_pass(p_ps[j][:], j, z, whole)
+        for c in range(4):
+            wb_pass(p_ps[0][:, chunks[c]], 0, chunks[c], c == 3)
+        wb_pass(p_ps[1][:], 1, whole, True)
+        for z in range(2):
+            wq_pass(p_ps[2][:], 2, z, whole)
+        wb_pass(p_ps[2][:], 2, whole, True)
+        p_last = [ps.tile([P, CH], F32, name="p_last%d" % c, tag="chunk%d" % c) for c in range(4)]
+        for c in range(4):
+            for z in range(2):
+                wq_pass(p_last[c][:], 3, z, chunks[c])
+            wb_pass(p_last[c][:], 3, chunks[c], True)
 
         out_rows = out_0.rearrange("(p j) t -> p j t", j=PACK)
 
-        def squash(j, cols):
+        def squash(acc, j, cols):
             nc.vector.tensor_tensor(
-                out=rest[j][:, cols], in0=tg_sb[j // 2][:, j % 2, cols], in1=p_ps[j][:, cols], op=ALU.subtract
+                out=rest[j][:, cols], in0=tg_of[j][:, cols], in1=acc, op=ALU.subtract
             )
             nc.scalar.activation(out=y[:, j, cols], in_=rest[j][:, cols], func=ACT.Tanh)
 
         for j in range(PACK - 1):
-            squash(j, slice(0, T))
+            for cols in halves:
+                squash(p_ps[j][:, cols], j, cols)
             nc.sync.dma_start(out=out_rows[:, j, :], in_=y[:, j, :])
-        for cols in (slice(0, CH), slice(CH, 2 * CH), slice(2 * CH, T)):
-            squash(PACK - 1, cols)
+        for c in range(4):
+            squash(p_last[c][:], PACK - 1, chunks[c])
         nc.sync.dma_start(out=out_rows[:, PACK - 1, :], in_=y[:, PACK - 1, :])
 
         def round_views(c):

from contextlib import ExitStack

import concourse.mybir as mybir

K, L, T, R, N = 1024, 1024, 512, 512, 512
FLOPS = 2 * T * (K * R + R * N + L * N)

F32 = mybir.dt.float32
BF16 = mybir.dt.bfloat16
I32 = mybir.dt.int32
U8 = mybir.dt.uint8
FP8X4 = mybir.dt.float8_e4m3fn_x4
FP4X4 = mybir.dt.float4_e2m1fn_x4
ACT = mybir.ActivationFunctionType
ALU = mybir.AluOpType

P = 128
PACK = 4
W = 512
CH = 128


def tile_mix_unexplained_rest_pl_kernel(
    tc, xt_words, xt_scales, wa_words, wa_scales, wb_words, wb_scales,
    xq_words, xq_scales, wq_words, wq_scales, tg, out_0, out_1, out_2,
):
    nc = tc.nc
    with ExitStack() as ctx:
        sb = ctx.enter_context(tc.tile_pool(name="sb", bufs=1))
        ps = ctx.enter_context(tc.psum_pool(name="ps", bufs=1))
        ctx.enter_context(tc.manual_schedule())

        def tile(name, shape, dtype):
            return sb.tile(shape, dtype, name=name, align_bytes=64)

        wa_w_raw = [tile("wa_w_raw%d" % z, [P, 1, W], I32) for z in range(2)]
        wa_w = [tile("wa_w%d" % z, [P, W], I32) for z in range(2)]
        wa_s_raw = tile("wa_s_raw", [P, 2, W], U8)
        wa_s = tile("wa_s", [P, 2, W], U8)
        xt_w = tile("xt_w", [P, 2, 2 * W], U8)
        xt_s = tile("xt_s", [P, 2, W], U8)
        wq_w_raw = tile("wq_w_raw", [P, 2, 2 * W], U8)
        wq_w = [tile("wq_w%d" % z, [P, 2 * W], U8) for z in range(2)]
        wq_s_raw = tile("wq_s_raw", [P, 2, W], U8)
        wq_s = tile("wq_s", [P, 2, W], U8)
        xq_w = tile("xq_w", [P, 2, W], I32)
        xq_s = tile("xq_s", [P, 2, W], U8)
        wb_w_raw = tile("wb_w_raw", [P, 1, 2 * W], U8)
        wb_w = tile("wb_w", [P, 2 * W], U8)
        wb_s_raw = tile("wb_s_raw", [P, 1, W], U8)
        wb_s = tile("wb_s", [P, 1, W], U8)
        tg_sb = [tile("tg%d" % h, [P, rows, T], F32) for h, rows in enumerate((2, 1, 1))]
        tg_of = [tg_sb[0][:, 0, :], tg_sb[0][:, 1, :], tg_sb[1][:, 0, :], tg_sb[2][:, 0, :]]
        hid = [tile("hid%d" % c, [P, CH, PACK], BF16) for c in range(4)]
        hid_w = tile("hid_w", [P, T], I32)
        hid_s = tile("hid_s", [P, T], U8)
        rest = [tile("rest%d" % j, [P, T], F32) for j in range(PACK)]
        y = tile("y", [P, PACK, T], F32)
        y_bf = [tile("y_bf%d" % h, [P, T // 2, PACK], BF16) for h in range(2)]
        y_w = tile("y_w", [P, T], I32)
        y_s = tile("y_s", [P, T], U8)
        warm = tile("warm", [P, 8], F32)

        a_ps = [ps.tile([P, PACK, CH], F32, name="a_ps%d" % c, tag="chunk%d" % c) for c in range(4)]
        p_ps = [ps.tile([P, T], F32, name="p_ps%d" % j) for j in range(PACK - 1)]

        def zero(plane):
            nc.vector.memset(plane[:].bitcast(I32), 0)

        def load_scale_rows(queue, plane, scales, q):
            queue.dma_start(
                out=plane[32 * q : 32 * q + 4, :, :].bitcast(I32),
                in_=scales[:, 4 * q : 4 * q + 4, :].rearrange("z r c -> r z c").bitcast(I32),
            )

        def load_fp8_words(dst, words):
            nc.sync.dma_start(out=dst[:], in_=words.rearrange("z p c b -> p z (c b)").bitcast(I32))

        def load_fp4_words(dst, words):
            nc.sync.dma_start(out=dst[:].bitcast(I32), in_=words.rearrange("z p c -> p z c").bitcast(I32))

        def deal_scales(dst, src):
            nc.vector.tensor_copy(
                out=dst[:].rearrange("p z (j m) -> p z j m", j=PACK),
                in_=src[:].rearrange("p z (m j) -> p z j m", j=PACK),
            )

        def deal_fp8_words(dst, src):
            nc.vector.tensor_copy(
                out=dst.rearrange("p (j g i) -> p g j i", j=PACK, i=2),
                in_=src.rearrange("p (g i j) -> p g j i", j=PACK, i=2),
            )

        def deal_fp4_words(dst, src):
            nc.vector.tensor_copy(
                out=dst.rearrange("p (j m b) -> p j m b", j=PACK, b=2),
                in_=src.rearrange("p (m j b) -> p j m b", j=PACK, b=2),
            )

        nc.gpsimd.memset(wq_s_raw[:].bitcast(I32), 0)
        for plane in (wa_s_raw, xt_s, wb_s_raw, xq_s):
            zero(plane)
        nc.vector.memset(warm[:], 0.0)
        load_fp8_words(wa_w_raw[0], wa_words[0:1])
        for q in range(4):
            load_scale_rows(nc.sync if q < 2 else nc.scalar, wa_s_raw, wa_scales, q)
        load_fp8_words(wa_w_raw[1], wa_words[1:2])
        load_fp4_words(xt_w, xt_words)
        load_fp4_words(wq_w_raw, wq_words)
        nc.scalar.activation(out=warm[:, 4:5], in_=warm[:, 0:1], func=ACT.Tanh)
        for q in range(2, 4):
            load_scale_rows(nc.gpsimd, wq_s_raw, wq_scales, q)
        for q in range(2):
            load_scale_rows(nc.gpsimd, wb_s_raw, wb_scales, q)
        for q in range(4):
            load_scale_rows(nc.sync if q < 3 else nc.scalar, xt_s, xt_scales, q)
        load_scale_rows(nc.scalar, wq_s_raw, wq_scales, 0)
        load_fp4_words(wb_w_raw, wb_words)
        load_scale_rows(nc.sync, wq_s_raw, wq_scales, 1)
        load_fp8_words(xq_w, xq_words)
        for q in range(4):
            load_scale_rows(nc.sync, xq_s, xq_scales, q)
        for q in range(2, 4):
            load_scale_rows(nc.sync, wb_s_raw, wb_scales, q)
        tg_rows = tg.rearrange("(p j) t -> p j t", j=PACK)
        nc.sync.dma_start(out=tg_sb[0][:], in_=tg_rows[:, 0:2, :])
        nc.sync.dma_start(out=tg_sb[1][:], in_=tg_rows[:, 2:3, :])
        nc.sync.dma_start(out=tg_sb[2][:], in_=tg_rows[:, 3:4, :])

        for i in range(11):
            nc.tensor.matmul_mx(
                out=a_ps[3][:, i % PACK, :],
                lhsT=wa_w_raw[0][:, 0, 0:P].bitcast(FP8X4),
                lhsT_scale=wa_s_raw[:, 0, 0:P],
                rhs=wa_w_raw[0][:, 0, P : P + CH // 2].bitcast(U8).bitcast(FP4X4),
                rhs_scale=wa_s_raw[:, 0, P : P + CH],
                start=True,
                stop=True,
            )

        deal_fp8_words(wa_w[0][:], wa_w_raw[0][:, 0, :])
        deal_scales(wa_s, wa_s_raw)
        deal_fp8_words(wa_w[1][:], wa_w_raw[1][:, 0, :])
        for c in range(4):
            for z in range(2):
                for j in range(PACK):
                    nc.tensor.matmul_mx(
                        out=a_ps[c][:, j, :],
                        lhsT=wa_w[z][:, P * j : P * (j + 1)].bitcast(FP8X4),
                        lhsT_scale=wa_s[:, z, P * j : P * (j + 1)],
                        rhs=xt_w[:, z, 2 * CH * c : 2 * CH * (c + 1)].bitcast(FP4X4),
                        rhs_scale=xt_s[:, z, CH * c : CH * (c + 1)],
                        start=(z == 0 and j == 0),
                        stop=(z == 1 and j == PACK - 1),
                    )
            nc.scalar.activation(out=hid[c][:], in_=a_ps[c][:].rearrange("p j t -> p t j"), func=ACT.Relu)

        def quantize_hid(c):
            nc.vector.quantize_mx(
                out=hid_w[:, CH * c : CH * (c + 1)].bitcast(FP8X4),
                scales=hid_s[:, CH * c : CH * (c + 1)],
                in_=hid[c][:].rearrange("p t j -> p (t j)"),
            )

        deal_fp4_words(wq_w[0][:], wq_w_raw[:, 0, :])
        deal_fp4_words(wq_w[1][:], wq_w_raw[:, 1, :])
        deal_fp4_words(wb_w[:], wb_w_raw[:, 0, :])
        deal_scales(wq_s, wq_s_raw)
        quantize_hid(0)
        quantize_hid(1)
        quantize_hid(2)
        deal_scales(wb_s, wb_s_raw)
        quantize_hid(3)

        def wq_pass(acc, j, z, cols):
            nc.tensor.matmul_mx(
                out=acc,
                lhsT=wq_w[z][:, 2 * P * j : 2 * P * (j + 1)].bitcast(FP4X4),
                lhsT_scale=wq_s[:, z, P * j : P * (j + 1)],
                rhs=xq_w[:, z, cols].bitcast(FP8X4),
                rhs_scale=xq_s[:, z, cols],
                start=(z == 0),
                stop=False,
            )

        def wb_pass(acc, j, cols, stop):
            nc.tensor.matmul_mx(
                out=acc,
                lhsT=wb_w[:, 2 * P * j : 2 * P * (j + 1)].bitcast(FP4X4),
                lhsT_scale=wb_s[:, 0, P * j : P * (j + 1)],
                rhs=hid_w[:, cols].bitcast(FP8X4),
                rhs_scale=hid_s[:, cols],
                start=False,
                stop=stop,
            )

        whole = slice(0, T)
        halves = [slice(0, T // 2), slice(T // 2, T)]
        chunks = [slice(CH * c, CH * (c + 1)) for c in range(4)]
        for z in range(2):
            for j in range(2):
                wq_pass(p_ps[j][:], j, z, whole)
        for c in range(4):
            wb_pass(p_ps[0][:, chunks[c]], 0, chunks[c], c == 3)
        wb_pass(p_ps[1][:], 1, whole, True)
        for z in range(2):
            wq_pass(p_ps[2][:], 2, z, whole)
        wb_pass(p_ps[2][:], 2, whole, True)
        p_last = [ps.tile([P, CH], F32, name="p_last%d" % c, tag="chunk%d" % c) for c in range(4)]
        for c in range(4):
            for z in range(2):
                wq_pass(p_last[c][:], 3, z, chunks[c])
            wb_pass(p_last[c][:], 3, chunks[c], True)

        out_rows = out_0.rearrange("(p j) t -> p j t", j=PACK)

        def squash(acc, j, cols):
            nc.vector.tensor_tensor(
                out=rest[j][:, cols], in0=tg_of[j][:, cols], in1=acc, op=ALU.subtract
            )
            nc.scalar.activation(out=y[:, j, cols], in_=rest[j][:, cols], func=ACT.Tanh)

        for j in range(PACK - 1):
            for cols in halves:
                squash(p_ps[j][:, cols], j, cols)
            nc.sync.dma_start(out=out_rows[:, j, :], in_=y[:, j, :])
        for c in range(4):
            squash(p_last[c][:], PACK - 1, chunks[c])
        nc.sync.dma_start(out=out_rows[:, PACK - 1, :], in_=y[:, PACK - 1, :])

        def round_views(c):
            dst = y_bf[c // 2][:, CH * (c % 2) : CH * (c % 2 + 1), :].rearrange("p (g i) j -> p g j i", i=4)
            src = y[:, :, CH * c : CH * (c + 1)].rearrange("p j (g i) -> p g j i", i=4)
            return dst, src

        def quantize_y(h):
            cols = slice(h * T // 2, (h + 1) * T // 2)
            nc.vector.quantize_mx(
                out=y_w[:, cols].bitcast(FP8X4), scales=y_s[:, cols], in_=y_bf[h][:].rearrange("p t j -> p (t j)")
            )

        out_words = out_1.rearrange("z p c b -> p (z c b)").bitcast(I32)
        for c in range(3):
            dst, src = round_views(c)
            nc.vector.tensor_copy(out=dst, in_=src)
        dst, src = round_views(3)
        nc.scalar.copy(out=dst, in_=src)
        for h in range(2):
            quantize_y(h)
            cols = slice(h * T // 2, (h + 1) * T // 2)
            nc.sync.dma_start(out=out_words[:, cols], in_=y_w[:, cols])
        for q in range(4):
            queue = nc.scalar if q % 2 == 0 else nc.sync
            queue.dma_start(
                out=out_2[0, 4 * q : 4 * q + 4, :].bitcast(I32), in_=y_s[32 * q : 32 * q + 4, :].bitcast(I32)
            )
